import numpy as np
import ml_dtypes


def mxq(x, axis, fmt="e4m3"):
    dtype, down = {"e4m3": (ml_dtypes.float8_e4m3fn, 7), "e5m2": (ml_dtypes.float8_e5m2, 14)}[fmt]
    v = np.moveaxis(np.asarray(x, np.float32).astype(ml_dtypes.bfloat16).astype(np.float64), axis, -1)
    blocks = v.reshape(v.shape[:-1] + (-1, 32))
    amax = np.abs(blocks).max(-1, keepdims=True)
    byte = np.maximum(np.where(amax > 0, np.frexp(amax)[1] - 1 + 127, 0) - down, 1)
    scale = np.exp2(byte - 127.0)
    codes = (blocks / scale).astype(np.float32).astype(dtype).astype(np.float64)
    return np.moveaxis((codes * scale).reshape(v.shape), -1, axis)


WIDE = False


def mx_kscale(k):
    if not WIDE:
        return np.ones(k)
    levels = np.array([10, -10, 5, -5, 0])
    if k % 512:
        return np.exp2(np.random.permutation(np.resize(levels, k // 32))).repeat(32)
    a = np.empty((k // 512, 16))
    for p in range(k // 512):
        a[p, :8] = np.random.permutation(np.resize(levels, 8))
        for g in range(8):
            far = levels[np.abs(levels - a[p, g]) >= 10]
            a[p, g + 8] = far[np.random.randint(len(far))]
    return np.exp2(a.ravel()).repeat(32)


def f64(x):
    return np.asarray(x).astype(np.float64)


def striped(idx):
    return np.tile(np.asarray(idx).reshape(-1, 16).T, (8, 1)).astype(np.uint16)


def unstriped(offs):
    return offs[:16].T.reshape(-1).astype(np.int64)


E2M1 = np.array([0.0, 0.5, 1.0, 1.5, 2.0, 3.0, 4.0, 6.0, -0.0, -0.5, -1.0, -1.5, -2.0, -3.0, -4.0, -6.0])


def pack_weight(w, fmt):
    k, n = w.shape
    w = f64(np.asarray(w, np.float32).astype(ml_dtypes.bfloat16)).reshape(k // 32, 32, n)
    amax = np.abs(w).max(1)
    if fmt == "e4m3":
        byte = np.frexp(amax)[1] - 1 + 127 - 7
    else:
        mant, ex = np.frexp(amax / 6.0)
        byte = np.where(mant > 0.5, ex, ex - 1) + 127
    byte = np.clip(np.where(amax > 0, byte, 1), 1, 254)
    scaled = (w * np.exp2(127.0 - byte)[:, None, :]).reshape(k, n).astype(np.float32)
    by_word = np.ascontiguousarray(scaled.reshape(k // 512, 128, 4, n).transpose(0, 1, 3, 2))
    if fmt == "e4m3":
        words = by_word.astype(ml_dtypes.float8_e4m3fn).view(np.uint8)
    else:
        c = by_word.astype(ml_dtypes.float4_e2m1fn).view(np.uint8) & 0xF
        words = (c[..., 0::2] | (c[..., 1::2] << 4)).reshape(k // 512, 128, 2 * n)
    return np.ascontiguousarray(words), np.ascontiguousarray(byte.astype(np.uint8).reshape(k // 512, 16, n))


def unpack_weight(words, scales, fmt):
    g, _, n = scales.shape
    words = np.ascontiguousarray(words).reshape(g, 128, n, -1)
    if fmt == "e4m3":
        vals = words.view(ml_dtypes.float8_e4m3fn).astype(np.float64)
    else:
        nib = np.empty((g, 128, n, 4), np.uint8)
        nib[..., 0::2] = words & 0xF
        nib[..., 1::2] = words >> 4
        vals = E2M1[nib]
    vals = vals * np.repeat(np.exp2(scales.astype(np.float64) - 127.0), 8, axis=1)[..., None]
    return vals.transpose(0, 1, 3, 2).reshape(g * 512, n)


def softplus(v):
    return np.log(1.0 + np.exp(v))


def sigmoid(v):
    return 1.0 / (1.0 + np.exp(-v))


D, K, R, T, I, Q = 512, 512, 512, 2048, 512, 128


def setup_inputs():
    n = np.random.standard_normal
    idx = np.random.permutation(T)[:I]
    fd = mx_kscale(D)
    fk = mx_kscale(K)
    fr = mx_kscale(R)
    keysp = pack_weight(n((D, T)) / fd[:, None], "e2m1")
    tabp = pack_weight(n((K, T)) / fk[:, None], "e2m1")
    return {
        "query": (n((D, Q)) * 0.9 / np.sqrt(D) * fd[:, None]).astype(np.float32),
        "keys_words": keysp[0],
        "keys_scales": keysp[1],
        "th": (np.random.uniform(-0.3, 0.6, (Q, 1))).astype(np.float32),
        "reserve": (np.random.uniform(50.0, 200.0, (Q, 1))).astype(np.float32),
        "tab_words": tabp[0],
        "tab_scales": tabp[1],
        "w1": (n((K, R)) * 1 / np.sqrt(K) * fk[:, None]).astype(np.float32),
        "gain": (np.random.uniform(0.5, 2.0, (R, 1))).astype(np.float32),
        "gout": (n((R, Q)) * 1 / np.sqrt(R) * fr[:, None]).astype(np.float32),
        "hsc": (np.random.uniform(0.7, 1.4, (R, 1)) / fr[:, None]).astype(np.float32),
        "old": (0.5 * n((Q, T))).astype(np.float32),
        "offs": striped(idx),
    }


def reference(query, keys_words, keys_scales, th, reserve, tab_words, tab_scales, w1, gain, gout, hsc, old, offs):
    idx = unstriped(offs)
    keysu = unpack_weight(keys_words, keys_scales, "e2m1")
    tabu = unpack_weight(tab_words, tab_scales, "e2m1")
    queryq = mxq(f64(query), 0, "e4m3")
    keysidxg = keysu[:, idx]
    a = queryq.T @ keysidxg
    p = softplus(a - f64(th))
    z = np.sum(p, axis=1, keepdims=True) + f64(reserve)
    w1q = mxq(f64(w1), 0, "e4m3")
    tabidxg = tabu[:, idx]
    zh = w1q.T @ tabidxg
    ht = np.tanh(zh)
    hv = ht * f64(gain)
    hs1 = hv * f64(hsc)
    goutq = mxq(f64(gout), 0, "e4m3")
    hs1q = mxq(hs1, 0, "e4m3")
    c0 = goutq.T @ hs1q
    dz = np.sum(c0 * p / np.square(z) * (-1.0), axis=1, keepdims=True)
    dp = c0 / z + dz
    da = dp * sigmoid(a - f64(th))
    gs = da * 512.0
    gf = np.zeros((Q, T))
    gf[:, idx] = gs
    y = f64(old) + gf
    return y

@@ -1,0 +1,196 @@
+from contextlib import ExitStack
+
+import concourse.mybir as mybir
+
+D, K, R, T, I, Q = 512, 512, 512, 2048, 512, 128
+FLOPS = 2 * (D * Q * I + K * R * I + R * Q * I)
+
+F32 = mybir.dt.float32
+BF16 = mybir.dt.bfloat16
+I32 = mybir.dt.int32
+U32 = mybir.dt.uint32
+U16 = mybir.dt.uint16
+U8 = mybir.dt.uint8
+FP8X4 = mybir.dt.float8_e4m3fn_x4
+FP4X4 = mybir.dt.float4_e2m1fn_x4
+ACT = mybir.ActivationFunctionType
+ALU = mybir.AluOpType
+
+P = 128
+PACK = 4
+CHUNK = 128
+CHUNKS = I // CHUNK
+OUT_COLS = 512
+
+
+def tile_attend_blrgained_capped_kernel(tc, query, keys_words, keys_scales, th, reserve, tab_words, tab_scales,
+                                         w1, gain, gout, hsc, old, offs, out):
+    nc = tc.nc
+    with ExitStack() as ctx:
+        sb = ctx.enter_context(tc.tile_pool(name="sb", bufs=1))
+        ps = ctx.enter_context(tc.psum_pool(name="ps", bufs=1))
+
+        def tile(name, shape, dtype):
+            return sb.tile(shape, dtype, name=name, align_bytes=64)
+
+        offsets = tile("offsets", [P, I // 16], U16)
+        nc.sync.dma_start(offsets[:], offs)
+
+        tab_scale_pool = tile("tab_scale_pool", [P, T], U8)
+        key_scale_pool = tile("key_scale_pool", [P, T], U8)
+        window = tile("window", [P, T], F32)
+        nc.vector.memset(tab_scale_pool[:].bitcast(I32), 0)
+        nc.vector.memset(key_scale_pool[:].bitcast(I32), 0)
+        nc.vector.memset(window[:], 0.0)
+
+        def load_scales(queue, pool_tile, scales):
+            for quad in range(4):
+                queue.dma_start(pool_tile[32 * quad:32 * quad + 4, :].bitcast(I32),
+                                scales[0, 4 * quad:4 * quad + 4, :].bitcast(I32))
+
+        tab_word_pool = tile("tab_word_pool", [P, T], U16)
+        nc.sync.dma_start(tab_word_pool[:].bitcast(I32), tab_words[0].bitcast(I32))
+        load_scales(nc.scalar, tab_scale_pool, tab_scales)
+        w_rows = w1.rearrange("(p j) c -> p j c", j=PACK)
+        w_raw = [tile("w_raw%d" % h, [P, PACK, R // 2], F32) for h in range(2)]
+        for h in range(2):
+            nc.sync.dma_start(w_raw[h][:], w_rows[:, :, h * (R // 2):(h + 1) * (R // 2)])
+        q_raw = tile("q_raw", [P, PACK, Q], F32)
+        nc.sync.dma_start(q_raw[:], query.rearrange("(p j) c -> p j c", j=PACK))
+        key_word_pool = tile("key_word_pool", [P, T], U16)
+        nc.sync.dma_start(key_word_pool[:].bitcast(I32), keys_words[0].bitcast(I32))
+        load_scales(nc.sync, key_scale_pool, keys_scales)
+        g_raw = tile("g_raw", [P, PACK, Q], F32)
+        nc.sync.dma_start(g_raw[:], gout.rearrange("(p j) c -> p j c", j=PACK))
+        old_sb = tile("old_sb", [P, T], F32)
+        nc.sync.dma_start(old_sb[:], old)
+
+        th_col = tile("th_col", [P, 1], F32)
+        reserve_col = tile("reserve_col", [P, 1], F32)
+        gain_cols = tile("gain_cols", [P, PACK], F32)
+        hsc_cols = tile("hsc_cols", [P, PACK], F32)
+        nc.gpsimd.dma_start(gain_cols[:], gain.rearrange("(p t) o -> p (t o)", t=PACK))
+        nc.gpsimd.dma_start(hsc_cols[:], hsc.rearrange("(p t) o -> p (t o)", t=PACK))
+        nc.gpsimd.dma_start(th_col[:], th)
+        nc.gpsimd.dma_start(reserve_col[:], reserve)
+        feature_scale = tile("feature_scale", [P, PACK], F32)
+        nc.gpsimd.tensor_tensor(feature_scale[:], gain_cols[:], hsc_cols[:], ALU.mult)
+        neg_th = tile("neg_th", [P, 1], F32)
+        neg_half_th = tile("neg_half_th", [P, 1], F32)
+        nc.gpsimd.tensor_scalar(neg_th[:], th_col[:], -1.0, 0.0, ALU.mult, ALU.add)
+        nc.gpsimd.tensor_scalar(neg_half_th[:], th_col[:], -0.5, 0.0, ALU.mult, ALU.add)
+
+        tab_w = tile("tab_w", [P, I], U16)
+        tab_s = tile("tab_s", [P, I], U8)
+        nc.vector.tensor_copy(tab_w[:], tab_word_pool[:].indirect(offsets[:]))
+        nc.vector.tensor_copy(tab_s[:], tab_scale_pool[:].indirect(offsets[:]))
+
+        w_bf = tile("w_bf", [P, PACK, P, PACK], BF16)
+        half = P // 2
+        w_dst = [w_bf[:, :, h * half:(h + 1) * half, :].rearrange("p t m j -> p m t j") for h in range(2)]
+        w_src = [w_raw[h][:].rearrange("p j (m t) -> p m t j", t=PACK) for h in range(2)]
+        nc.scalar.activation(w_dst[0], w_src[0], ACT.Copy)
+        nc.vector.tensor_copy(w_dst[1], w_src[1])
+        w_codes = tile("w_codes", [P, R], U32)
+        w_scales = tile("w_scales", [P, R], U8)
+        nc.vector.quantize_mx(out=w_codes[:].bitcast(FP8X4), scales=w_scales[:],
+                              in_=w_bf[:].rearrange("p t m j -> p (t m j)"))
+
+        def interleaved_views(dst, src):
+            return (dst[:].rearrange("p (c i) j -> p c j i", i=PACK), src[:].rearrange("p j (c i) -> p c j i", i=PACK))
+
+        q_bf = tile("q_bf", [P, Q, PACK], BF16)
+        q_dst, q_src = interleaved_views(q_bf, q_raw)
+        nc.scalar.activation(q_dst, q_src, ACT.Copy)
+        q_codes = tile("q_codes", [P, Q], U32)
+        q_scales = tile("q_scales", [P, Q], U8)
+        nc.vector.quantize_mx(out=q_codes[:].bitcast(FP8X4), scales=q_scales[:],
+                              in_=q_bf[:].rearrange("p c j -> p (c j)"))
+
+        ht = []
+        for c in range(CHUNKS):
+            cols = slice(c * CHUNK, (c + 1) * CHUNK)
+            zh = ps.tile([P, PACK, CHUNK], F32, name="zh%d" % c)
+            for t in range(PACK):
+                rows = slice(t * P, (t + 1) * P)
+                nc.tensor.matmul_mx(out=zh[:, t, :], lhsT=w_codes[:, rows].bitcast(FP8X4), lhsT_scale=w_scales[:, rows],
+                                    rhs=tab_w[:, cols].bitcast(FP4X4), rhs_scale=tab_s[:, cols], start=True, stop=True)
+            ht_c = tile("ht%d" % c, [P, CHUNK, PACK], F32)
+            nc.scalar.activation(ht_c[:], zh[:].rearrange("p t n -> p n t"), ACT.Tanh)
+            ht.append(ht_c)
+
+        key_w = tile("key_w", [P, I], U16)
+        key_s = tile("key_s", [P, I], U8)
+        nc.vector.tensor_copy(key_w[:], key_word_pool[:].indirect(offsets[:]))
+        nc.vector.tensor_copy(key_s[:], key_scale_pool[:].indirect(offsets[:]))
+        a = ps.tile([P, I], F32, name="a")
+        nc.tensor.matmul_mx(out=a[:], lhsT=q_codes[:].bitcast(FP8X4), lhsT_scale=q_scales[:],
+                            rhs=key_w[:].bitcast(FP4X4), rhs_scale=key_s[:], start=True, stop=True)
+
+        half_tanh = tile("half_tanh", [P, I], F32)
+        abs_tanh = tile("abs_tanh", [P, I], F32)
+        relu_x = tile("relu_x", [P, I], F32)
+        log_sig = tile("log_sig", [P, I], F32)
+        sig512 = tile("sig512", [P, I], F32)
+        relu_sum = tile("relu_sum", [P, 1], F32)
+        log_sum = tile("log_sum", [P, 1], F32)
+        nc.scalar.activation(half_tanh[:], a[:], ACT.Tanh, bias=neg_half_th[:], scale=0.5)
+        nc.scalar.activation(abs_tanh[:], half_tanh[:], ACT.Abs)
+        nc.scalar.activation(relu_x[:], a[:], ACT.Relu, bias=neg_th[:], accum_out=relu_sum[:])
+        nc.scalar.activation(log_sig[:], abs_tanh[:], ACT.Ln, bias=0.5, scale=0.5, accum_out=log_sum[:])
+        nc.scalar.activation(sig512[:], half_tanh[:], ACT.Identity, bias=256.0, scale=256.0)
+
+        g_bf = tile("g_bf", [P, Q, PACK], BF16)
+        g_dst, g_src = interleaved_views(g_bf, g_raw)
+        nc.vector.tensor_copy(g_dst, g_src)
+        g_codes = tile("g_codes", [P, Q], U32)
+        g_scales = tile("g_scales", [P, Q], U8)
+        nc.vector.quantize_mx(out=g_codes[:].bitcast(FP8X4), scales=g_scales[:],
+                              in_=g_bf[:].rearrange("p c j -> p (c j)"))
+
+        c0 = ps.tile([P, I], F32, name="c0")
+        scale_by_place = feature_scale[:].unsqueeze(1).to_broadcast([P, CHUNK, PACK])
+        hs = [tile("hs%d" % c, [P, CHUNK, PACK], BF16) for c in range(CHUNKS)]
+
+        def scale_chunk(c):
+            nc.vector.tensor_tensor(hs[c][:], ht[c][:], scale_by_place, ALU.mult)
+
+        def multiply_chunk(c):
+            h_codes = tile("h_codes%d" % c, [P, CHUNK], U32)
+            h_scales = tile("h_scales%d" % c, [P, CHUNK], U8)
+            nc.vector.quantize_mx(out=h_codes[:].bitcast(FP8X4), scales=h_scales[:],
+                                  in_=hs[c][:].rearrange("p n t -> p (n t)"))
+            nc.tensor.matmul_mx(out=c0[:, c * CHUNK:(c + 1) * CHUNK], lhsT=g_codes[:].bitcast(FP8X4),
+                                lhsT_scale=g_scales[:], rhs=h_codes[:].bitcast(FP8X4), rhs_scale=h_scales[:],
+                                start=True, stop=True)
+
+        scale_chunk(0)
+        for c in range(1, CHUNKS):
+            scale_chunk(c)
+            multiply_chunk(c - 1)
+        multiply_chunk(CHUNKS - 1)
+
+        prod_relu = tile("prod_relu", [P, I], F32)
+        prod_log = tile("prod_log", [P, I], F32)
+        s_relu = tile("s_relu", [P, 1], F32)
+        s_log = tile("s_log", [P, 1], F32)
+        z = tile("z", [P, 1], F32)
+        rz = tile("rz", [P, 1], F32)
+        shift = tile("shift", [P, 1], F32)
+        nc.vector.scalar_tensor_tensor(prod_relu[:], c0[:], 1.0, relu_x[:], ALU.mult, ALU.mult, accum_out=s_relu[:])
+        nc.vector.tensor_scalar(z[:], relu_sum[:], reserve_col[:], log_sum[:], ALU.add, ALU.subtract)
+        nc.vector.scalar_tensor_tensor(prod_log[:], c0[:], 1.0, log_sig[:], ALU.mult, ALU.mult, accum_out=s_log[:])
+        nc.vector.reciprocal(rz[:], z[:])
+        nc.vector.tensor_scalar(shift[:], s_log[:], s_relu[:], rz[:], ALU.subtract, ALU.mult)
+        halves = [slice(h * (I // 2), (h + 1) * (I // 2)) for h in range(2)]
+        dp = [tile("dp%d" % h, [P, I // 2], F32) for h in range(2)]
+        for h in range(2):
+            nc.vector.tensor_scalar(dp[h][:], c0[:, halves[h]], shift[:], rz[:], ALU.add, ALU.mult)
+        for h in range(2):
+            nc.vector.tensor_tensor(window[:].indirect(offsets[:, h * 16:(h + 1) * 16]), dp[h][:],
+                                    sig512[:, halves[h]], ALU.mult)
+        for c in range(T // OUT_COLS):
+            cols = slice(c * OUT_COLS, (c + 1) * OUT_COLS)
+            result = tile("result%d" % c, [P, OUT_COLS], F32)
+            nc.vector.tensor_tensor(result[:], window[:, cols], old_sb[:, cols], ALU.add)
+            nc.sync.dma_start(out[:, cols], result[:])

@@ -20,7 +20,7 @@ P = 128
 PACK = 4
 CHUNK = 128
 CHUNKS = I // CHUNK
-OUT_COLS = 512
+OUT_COLS = (256, 384, 384, 512, 512)
 
 
 def tile_attend_blrgained_capped_kernel(tc, query, keys_words, keys_scales, th, reserve, tab_words, tab_scales,
@@ -28,43 +28,39 @@ def tile_attend_blrgained_capped_kernel(tc, query, keys_words, keys_scales, th, 
     nc = tc.nc
     with ExitStack() as ctx:
         sb = ctx.enter_context(tc.tile_pool(name="sb", bufs=1))
+        reuse = ctx.enter_context(tc.tile_pool(name="reuse", bufs=1))
         ps = ctx.enter_context(tc.psum_pool(name="ps", bufs=1))
 
-        def tile(name, shape, dtype):
-            return sb.tile(shape, dtype, name=name, align_bytes=64)
-
-        offsets = tile("offsets", [P, I // 16], U16)
-        nc.sync.dma_start(offsets[:], offs)
+        def tile(name, shape, dtype, tag=None):
+            return sb.tile(shape, dtype, name=name, tag=tag or name, align_bytes=64)
 
         tab_scale_pool = tile("tab_scale_pool", [P, T], U8)
-        key_scale_pool = tile("key_scale_pool", [P, T], U8)
         window = tile("window", [P, T], F32)
+        zero_col = tile("zero_col", [P, 1], F32)
+        key_scale_pool = tile("key_scale_pool", [P, T], U8)
         nc.vector.memset(tab_scale_pool[:].bitcast(I32), 0)
         nc.vector.memset(key_scale_pool[:].bitcast(I32), 0)
         nc.vector.memset(window[:], 0.0)
+        nc.scalar.mul(zero_col[:].bitcast(U32), zero_col[:].bitcast(U32), 0.0)
 
-        def load_scales(queue, pool_tile, scales):
+        def load_scales(pool_tile, scales):
             for quad in range(4):
-                queue.dma_start(pool_tile[32 * quad:32 * quad + 4, :].bitcast(I32),
+                nc.sync.dma_start(pool_tile[32 * quad:32 * quad + 4, :].bitcast(I32),
                                 scales[0, 4 * quad:4 * quad + 4, :].bitcast(I32))
 
+        def overlaid(name, shape, dtype, offset):
+            return reuse.tile(shape, dtype, name=name, align_bytes=64, offset=offset)
+
+        offsets = tile("offsets", [P, I // 16], U16)
+        nc.sync.dma_start(offsets[:], offs)
         tab_word_pool = tile("tab_word_pool", [P, T], U16)
         nc.sync.dma_start(tab_word_pool[:].bitcast(I32), tab_words[0].bitcast(I32))
-        load_scales(nc.scalar, tab_scale_pool, tab_scales)
         w_rows = w1.rearrange("(p j) c -> p j c", j=PACK)
-        w_raw = [tile("w_raw%d" % h, [P, PACK, R // 2], F32) for h in range(2)]
+        w_raw = [overlaid("w_raw0", [P, PACK, R // 2], F32, 0), tile("w_raw1", [P, PACK, R // 2], F32)]
         for h in range(2):
             nc.sync.dma_start(w_raw[h][:], w_rows[:, :, h * (R // 2):(h + 1) * (R // 2)])
-        q_raw = tile("q_raw", [P, PACK, Q], F32)
-        nc.sync.dma_start(q_raw[:], query.rearrange("(p j) c -> p j c", j=PACK))
-        key_word_pool = tile("key_word_pool", [P, T], U16)
-        nc.sync.dma_start(key_word_pool[:].bitcast(I32), keys_words[0].bitcast(I32))
-        load_scales(nc.sync, key_scale_pool, keys_scales)
-        g_raw = tile("g_raw", [P, PACK, Q], F32)
-        nc.sync.dma_start(g_raw[:], gout.rearrange("(p j) c -> p j c", j=PACK))
-        old_sb = tile("old_sb", [P, T], F32)
-        nc.sync.dma_start(old_sb[:], old)
-
+        load_scales(tab_scale_pool, tab_scales)
+        load_scales(key_scale_pool, keys_scales)
         th_col = tile("th_col", [P, 1], F32)
         reserve_col = tile("reserve_col", [P, 1], F32)
         gain_cols = tile("gain_cols", [P, PACK], F32)
@@ -75,26 +71,44 @@ def tile_attend_blrgained_capped_kernel(tc, query, keys_words, keys_scales, th, 
         nc.gpsimd.dma_start(reserve_col[:], reserve)
         feature_scale = tile("feature_scale", [P, PACK], F32)
         nc.gpsimd.tensor_tensor(feature_scale[:], gain_cols[:], hsc_cols[:], ALU.mult)
-        neg_th = tile("neg_th", [P, 1], F32)
         neg_half_th = tile("neg_half_th", [P, 1], F32)
-        nc.gpsimd.tensor_scalar(neg_th[:], th_col[:], -1.0, 0.0, ALU.mult, ALU.add)
         nc.gpsimd.tensor_scalar(neg_half_th[:], th_col[:], -0.5, 0.0, ALU.mult, ALU.add)
 
         tab_w = tile("tab_w", [P, I], U16)
-        tab_s = tile("tab_s", [P, I], U8)
         nc.vector.tensor_copy(tab_w[:], tab_word_pool[:].indirect(offsets[:]))
-        nc.vector.tensor_copy(tab_s[:], tab_scale_pool[:].indirect(offsets[:]))
+        q_raw = tile("q_raw", [P, PACK, Q], F32, "tab_word_pool")
+        nc.sync.dma_start(q_raw[:], query.rearrange("(p j) c -> p j c", j=PACK))
 
-        w_bf = tile("w_bf", [P, PACK, P, PACK], BF16)
         half = P // 2
-        w_dst = [w_bf[:, :, h * half:(h + 1) * half, :].rearrange("p t m j -> p m t j") for h in range(2)]
-        w_src = [w_raw[h][:].rearrange("p j (m t) -> p m t j", t=PACK) for h in range(2)]
-        nc.scalar.activation(w_dst[0], w_src[0], ACT.Copy)
-        nc.vector.tensor_copy(w_dst[1], w_src[1])
-        w_codes = tile("w_codes", [P, R], U32)
-        w_scales = tile("w_scales", [P, R], U8)
-        nc.vector.quantize_mx(out=w_codes[:].bitcast(FP8X4), scales=w_scales[:],
-                              in_=w_bf[:].rearrange("p t m j -> p (t m j)"))
+        w_codes = tile("w_codes", [P, PACK, P], U32)
+        w_scales = tile("w_scales", [P, PACK, P], U8)
+
+        def cast_w(copy, name, tag, h, t0, t1):
+            w_bf = tile(name, [P, t1 - t0, half, PACK], BF16, tag)
+            copy(w_bf[:].rearrange("p t m j -> p m t j"),
+                 w_raw[h][:].rearrange("p j (m t) -> p m t j", t=PACK)[:, :, t0:t1, :])
+            return [(w_bf[:, t - t0, :, :], t, h) for t in range(t0, t1)]
+
+        def scalar_copy(dst, src):
+            nc.scalar.activation(dst, src, ACT.Copy)
+
+        pieces = cast_w(scalar_copy, "w_bf_first", None, 0, 0, PACK)
+        key_word_pool = overlaid("key_word_pool", [P, T], U16, 0)
+        nc.sync.dma_start(key_word_pool[:].bitcast(I32), keys_words[0].bitcast(I32))
+        pieces = pieces + cast_w(nc.vector.tensor_copy, "w_bf_vector", None, 1, 0, PACK - 1)
+        pieces = pieces + cast_w(scalar_copy, "w_bf_scalar", None, 1, PACK - 1, PACK)
+        for piece, t, h in pieces:
+            cols = slice(h * half, (h + 1) * half)
+            nc.vector.quantize_mx(out=w_codes[:, t, cols].bitcast(FP8X4), scales=w_scales[:, t, cols],
+                                  in_=piece.rearrange("p m j -> p (m j)"))
+        halves = [slice(h * (I // 2), (h + 1) * (I // 2)) for h in range(2)]
+        list_halves = [offsets[:, h * 16:(h + 1) * 16] for h in range(2)]
+        tab_s = tile("tab_s", [P, I], U8, "w_bf_scalar")
+        for h in range(2):
+            nc.vector.tensor_copy(tab_s[:, halves[h]], tab_scale_pool[:].indirect(list_halves[h]))
+
+        g_raw = tile("g_raw", [P, PACK, Q], F32, "w_raw1")
+        nc.sync.dma_start(g_raw[:], gout.rearrange("(p j) c -> p j c", j=PACK))
 
         def interleaved_views(dst, src):
             return (dst[:].rearrange("p (c i) j -> p c j i", i=PACK), src[:].rearrange("p j (c i) -> p c j i", i=PACK))
@@ -107,22 +121,19 @@ def tile_attend_blrgained_capped_kernel(tc, query, keys_words, keys_scales, th, 
         nc.vector.quantize_mx(out=q_codes[:].bitcast(FP8X4), scales=q_scales[:],
                               in_=q_bf[:].rearrange("p c j -> p (c j)"))
 
-        ht = []
+        ht = tile("ht", [P, CHUNKS, CHUNK, PACK], F32, "tab_word_pool")
         for c in range(CHUNKS):
             cols = slice(c * CHUNK, (c + 1) * CHUNK)
             zh = ps.tile([P, PACK, CHUNK], F32, name="zh%d" % c)
             for t in range(PACK):
-                rows = slice(t * P, (t + 1) * P)
-                nc.tensor.matmul_mx(out=zh[:, t, :], lhsT=w_codes[:, rows].bitcast(FP8X4), lhsT_scale=w_scales[:, rows],
+                nc.tensor.matmul_mx(out=zh[:, t, :], lhsT=w_codes[:, t, :].bitcast(FP8X4), lhsT_scale=w_scales[:, t, :],
                                     rhs=tab_w[:, cols].bitcast(FP4X4), rhs_scale=tab_s[:, cols], start=True, stop=True)
-            ht_c = tile("ht%d" % c, [P, CHUNK, PACK], F32)
-            nc.scalar.activation(ht_c[:], zh[:].rearrange("p t n -> p n t"), ACT.Tanh)
-            ht.append(ht_c)
+            nc.scalar.activation(ht[:, c, :, :], zh[:].rearrange("p t n -> p n t"), ACT.Tanh)
 
-        key_w = tile("key_w", [P, I], U16)
-        key_s = tile("key_s", [P, I], U8)
-        nc.vector.tensor_copy(key_w[:], key_word_pool[:].indirect(offsets[:]))
+        key_s = tile("key_s", [P, I], U8, "tab_scale_pool")
         nc.vector.tensor_copy(key_s[:], key_scale_pool[:].indirect(offsets[:]))
+        key_w = tile("key_w", [P, I], U16, "key_scale_pool")
+        nc.vector.tensor_copy(key_w[:], key_word_pool[:].indirect(offsets[:]))
         a = ps.tile([P, I], F32, name="a")
         nc.tensor.matmul_mx(out=a[:], lhsT=q_codes[:].bitcast(FP8X4), lhsT_scale=q_scales[:],
                             rhs=key_w[:].bitcast(FP4X4), rhs_scale=key_s[:], start=True, stop=True)
@@ -131,35 +142,33 @@ def tile_attend_blrgained_capped_kernel(tc, query, keys_words, keys_scales, th, 
         abs_tanh = tile("abs_tanh", [P, I], F32)
         relu_x = tile("relu_x", [P, I], F32)
         log_sig = tile("log_sig", [P, I], F32)
-        sig512 = tile("sig512", [P, I], F32)
         relu_sum = tile("relu_sum", [P, 1], F32)
         log_sum = tile("log_sum", [P, 1], F32)
         nc.scalar.activation(half_tanh[:], a[:], ACT.Tanh, bias=neg_half_th[:], scale=0.5)
         nc.scalar.activation(abs_tanh[:], half_tanh[:], ACT.Abs)
-        nc.scalar.activation(relu_x[:], a[:], ACT.Relu, bias=neg_th[:], accum_out=relu_sum[:])
         nc.scalar.activation(log_sig[:], abs_tanh[:], ACT.Ln, bias=0.5, scale=0.5, accum_out=log_sum[:])
+        sig512 = tile("sig512", [P, I], F32, "abs_tanh")
         nc.scalar.activation(sig512[:], half_tanh[:], ACT.Identity, bias=256.0, scale=256.0)
 
         g_bf = tile("g_bf", [P, Q, PACK], BF16)
-        g_dst, g_src = interleaved_views(g_bf, g_raw)
-        nc.vector.tensor_copy(g_dst, g_src)
-        g_codes = tile("g_codes", [P, Q], U32)
+        nc.gpsimd.tensor_copy(g_bf[:], g_raw[:].rearrange("p j c -> p c j"))
+        g_codes = overlaid("g_codes", [P, Q], U32, 0)
         g_scales = tile("g_scales", [P, Q], U8)
         nc.vector.quantize_mx(out=g_codes[:].bitcast(FP8X4), scales=g_scales[:],
                               in_=g_bf[:].rearrange("p c j -> p (c j)"))
 
         c0 = ps.tile([P, I], F32, name="c0")
         scale_by_place = feature_scale[:].unsqueeze(1).to_broadcast([P, CHUNK, PACK])
-        hs = [tile("hs%d" % c, [P, CHUNK, PACK], BF16) for c in range(CHUNKS)]
+        hs = [overlaid("hs%d" % c, [P, CHUNK, PACK], BF16, 4 * Q + 2 * PACK * CHUNK * c)[:] for c in range(CHUNKS)]
 
         def scale_chunk(c):
-            nc.vector.tensor_tensor(hs[c][:], ht[c][:], scale_by_place, ALU.mult)
+            nc.vector.tensor_tensor(hs[c], ht[:, c, :, :], scale_by_place, ALU.mult)
 
         def multiply_chunk(c):
             h_codes = tile("h_codes%d" % c, [P, CHUNK], U32)
             h_scales = tile("h_scales%d" % c, [P, CHUNK], U8)
             nc.vector.quantize_mx(out=h_codes[:].bitcast(FP8X4), scales=h_scales[:],
-                                  in_=hs[c][:].rearrange("p n t -> p (n t)"))
+                                  in_=hs[c].rearrange("p n t -> p (n t)"))
             nc.tensor.matmul_mx(out=c0[:, c * CHUNK:(c + 1) * CHUNK], lhsT=g_codes[:].bitcast(FP8X4),
                                 lhsT_scale=g_scales[:], rhs=h_codes[:].bitcast(FP8X4), rhs_scale=h_scales[:],
                                 start=True, stop=True)
@@ -170,6 +179,10 @@ def tile_attend_blrgained_capped_kernel(tc, query, keys_words, keys_scales, th, 
             multiply_chunk(c - 1)
         multiply_chunk(CHUNKS - 1)
 
+        old_sb = [tile("old_sb%d" % h, [P, T // 2], F32, tag) for h, tag in enumerate(("key_scale_pool", "tab_word_pool"))]
+        for h in range(2):
+            nc.sync.dma_start(old_sb[h][:], old[:, h * (T // 2):(h + 1) * (T // 2)])
+
         prod_relu = tile("prod_relu", [P, I], F32)
         prod_log = tile("prod_log", [P, I], F32)
         s_relu = tile("s_relu", [P, 1], F32)
@@ -177,20 +190,21 @@ def tile_attend_blrgained_capped_kernel(tc, query, keys_words, keys_scales, th, 
         z = tile("z", [P, 1], F32)
         rz = tile("rz", [P, 1], F32)
         shift = tile("shift", [P, 1], F32)
+        nc.vector.scalar_tensor_tensor(relu_x[:], a[:], th_col[:], zero_col[:].to_broadcast([P, I]), ALU.subtract, ALU.max,
+                                       accum_out=relu_sum[:])
         nc.vector.scalar_tensor_tensor(prod_relu[:], c0[:], 1.0, relu_x[:], ALU.mult, ALU.mult, accum_out=s_relu[:])
         nc.vector.tensor_scalar(z[:], relu_sum[:], reserve_col[:], log_sum[:], ALU.add, ALU.subtract)
         nc.vector.scalar_tensor_tensor(prod_log[:], c0[:], 1.0, log_sig[:], ALU.mult, ALU.mult, accum_out=s_log[:])
         nc.vector.reciprocal(rz[:], z[:])
         nc.vector.tensor_scalar(shift[:], s_log[:], s_relu[:], rz[:], ALU.subtract, ALU.mult)
-        halves = [slice(h * (I // 2), (h + 1) * (I // 2)) for h in range(2)]
         dp = [tile("dp%d" % h, [P, I // 2], F32) for h in range(2)]
         for h in range(2):
             nc.vector.tensor_scalar(dp[h][:], c0[:, halves[h]], shift[:], rz[:], ALU.add, ALU.mult)
         for h in range(2):
-            nc.vector.tensor_tensor(window[:].indirect(offsets[:, h * 16:(h + 1) * 16]), dp[h][:],
+            nc.vector.tensor_tensor(window[:].indirect(list_halves[h]), dp[h][:],
                                     sig512[:, halves[h]], ALU.mult)
-        for c in range(T // OUT_COLS):
-            cols = slice(c * OUT_COLS, (c + 1) * OUT_COLS)
-            result = tile("result%d" % c, [P, OUT_COLS], F32)
-            nc.vector.tensor_tensor(result[:], window[:, cols], old_sb[:, cols], ALU.add)
+        for c, width in enumerate(OUT_COLS):
+            cols = slice(sum(OUT_COLS[:c]), sum(OUT_COLS[:c + 1]))
+            result = tile("result%d" % c, [P, width], F32)
+            nc.vector.tensor_tensor(result[:], window[:, cols], old_sb[cols.start // (T // 2)][:, cols.start % (T // 2):(cols.stop - 1) % (T // 2) + 1], ALU.add)
             nc.sync.dma_start(out[:, cols], result[:])

from contextlib import ExitStack

import concourse.mybir as mybir

D, K, R, T, I, Q = 512, 512, 512, 2048, 512, 128
FLOPS = 2 * (D * Q * I + K * R * I + R * Q * I)

F32 = mybir.dt.float32
BF16 = mybir.dt.bfloat16
I32 = mybir.dt.int32
U32 = mybir.dt.uint32
U16 = mybir.dt.uint16
U8 = mybir.dt.uint8
FP8X4 = mybir.dt.float8_e4m3fn_x4
FP4X4 = mybir.dt.float4_e2m1fn_x4
ACT = mybir.ActivationFunctionType
ALU = mybir.AluOpType

P = 128
PACK = 4
CHUNK = 128
CHUNKS = I // CHUNK
OUT_COLS = (256, 384, 384, 512, 512)


def tile_attend_blrgained_capped_kernel(tc, query, keys_words, keys_scales, th, reserve, tab_words, tab_scales,
                                         w1, gain, gout, hsc, old, offs, out):
    nc = tc.nc
    with ExitStack() as ctx:
        sb = ctx.enter_context(tc.tile_pool(name="sb", bufs=1))
        reuse = ctx.enter_context(tc.tile_pool(name="reuse", bufs=1))
        ps = ctx.enter_context(tc.psum_pool(name="ps", bufs=1))

        def tile(name, shape, dtype, tag=None):
            return sb.tile(shape, dtype, name=name, tag=tag or name, align_bytes=64)

        tab_scale_pool = tile("tab_scale_pool", [P, T], U8)
        window = tile("window", [P, T], F32)
        zero_col = tile("zero_col", [P, 1], F32)
        key_scale_pool = tile("key_scale_pool", [P, T], U8)
        nc.vector.memset(tab_scale_pool[:].bitcast(I32), 0)
        nc.vector.memset(key_scale_pool[:].bitcast(I32), 0)
        nc.vector.memset(window[:], 0.0)
        nc.scalar.mul(zero_col[:].bitcast(U32), zero_col[:].bitcast(U32), 0.0)

        def load_scales(pool_tile, scales):
            for quad in range(4):
                nc.sync.dma_start(pool_tile[32 * quad:32 * quad + 4, :].bitcast(I32),
                                scales[0, 4 * quad:4 * quad + 4, :].bitcast(I32))

        def overlaid(name, shape, dtype, offset):
            return reuse.tile(shape, dtype, name=name, align_bytes=64, offset=offset)

        offsets = tile("offsets", [P, I // 16], U16)
        nc.sync.dma_start(offsets[:], offs)
        tab_word_pool = tile("tab_word_pool", [P, T], U16)
        nc.sync.dma_start(tab_word_pool[:].bitcast(I32), tab_words[0].bitcast(I32))
        w_rows = w1.rearrange("(p j) c -> p j c", j=PACK)
        w_raw = [overlaid("w_raw0", [P, PACK, R // 2], F32, 0), tile("w_raw1", [P, PACK, R // 2], F32)]
        for h in range(2):
            nc.sync.dma_start(w_raw[h][:], w_rows[:, :, h * (R // 2):(h + 1) * (R // 2)])
        load_scales(tab_scale_pool, tab_scales)
        load_scales(key_scale_pool, keys_scales)
        th_col = tile("th_col", [P, 1], F32)
        reserve_col = tile("reserve_col", [P, 1], F32)
        gain_cols = tile("gain_cols", [P, PACK], F32)
        hsc_cols = tile("hsc_cols", [P, PACK], F32)
        nc.gpsimd.dma_start(gain_cols[:], gain.rearrange("(p t) o -> p (t o)", t=PACK))
        nc.gpsimd.dma_start(hsc_cols[:], hsc.rearrange("(p t) o -> p (t o)", t=PACK))
        nc.gpsimd.dma_start(th_col[:], th)
        nc.gpsimd.dma_start(reserve_col[:], reserve)
        feature_scale = tile("feature_scale", [P, PACK], F32)
        nc.gpsimd.tensor_tensor(feature_scale[:], gain_cols[:], hsc_cols[:], ALU.mult)
        neg_half_th = tile("neg_half_th", [P, 1], F32)
        nc.gpsimd.tensor_scalar(neg_half_th[:], th_col[:], -0.5, 0.0, ALU.mult, ALU.add)

        tab_w = tile("tab_w", [P, I], U16)
        nc.vector.tensor_copy(tab_w[:], tab_word_pool[:].indirect(offsets[:]))
        q_raw = tile("q_raw", [P, PACK, Q], F32, "tab_word_pool")
        nc.sync.dma_start(q_raw[:], query.rearrange("(p j) c -> p j c", j=PACK))

        half = P // 2
        w_codes = tile("w_codes", [P, PACK, P], U32)
        w_scales = tile("w_scales", [P, PACK, P], U8)

        def cast_w(copy, name, tag, h, t0, t1):
            w_bf = tile(name, [P, t1 - t0, half, PACK], BF16, tag)
            copy(w_bf[:].rearrange("p t m j -> p m t j"),
                 w_raw[h][:].rearrange("p j (m t) -> p m t j", t=PACK)[:, :, t0:t1, :])
            return [(w_bf[:, t - t0, :, :], t, h) for t in range(t0, t1)]

        def scalar_copy(dst, src):
            nc.scalar.activation(dst, src, ACT.Copy)

        pieces = cast_w(scalar_copy, "w_bf_first", None, 0, 0, PACK)
        key_word_pool = overlaid("key_word_pool", [P, T], U16, 0)
        nc.sync.dma_start(key_word_pool[:].bitcast(I32), keys_words[0].bitcast(I32))
        pieces = pieces + cast_w(nc.vector.tensor_copy, "w_bf_vector", None, 1, 0, PACK - 1)
        pieces = pieces + cast_w(scalar_copy, "w_bf_scalar", None, 1, PACK - 1, PACK)
        for piece, t, h in pieces:
            cols = slice(h * half, (h + 1) * half)
            nc.vector.quantize_mx(out=w_codes[:, t, cols].bitcast(FP8X4), scales=w_scales[:, t, cols],
                                  in_=piece.rearrange("p m j -> p (m j)"))
        halves = [slice(h * (I // 2), (h + 1) * (I // 2)) for h in range(2)]
        list_halves = [offsets[:, h * 16:(h + 1) * 16] for h in range(2)]
        tab_s = tile("tab_s", [P, I], U8, "w_bf_scalar")
        for h in range(2):
            nc.vector.tensor_copy(tab_s[:, halves[h]], tab_scale_pool[:].indirect(list_halves[h]))

        g_raw = tile("g_raw", [P, PACK, Q], F32, "w_raw1")
        nc.sync.dma_start(g_raw[:], gout.rearrange("(p j) c -> p j c", j=PACK))

        def interleaved_views(dst, src):
            return (dst[:].rearrange("p (c i) j -> p c j i", i=PACK), src[:].rearrange("p j (c i) -> p c j i", i=PACK))

        q_bf = tile("q_bf", [P, Q, PACK], BF16)
        q_dst, q_src = interleaved_views(q_bf, q_raw)
        nc.scalar.activation(q_dst, q_src, ACT.Copy)
        q_codes = tile("q_codes", [P, Q], U32)
        q_scales = tile("q_scales", [P, Q], U8)
        nc.vector.quantize_mx(out=q_codes[:].bitcast(FP8X4), scales=q_scales[:],
                              in_=q_bf[:].rearrange("p c j -> p (c j)"))

        ht = tile("ht", [P, CHUNKS, CHUNK, PACK], F32, "tab_word_pool")
        for c in range(CHUNKS):
            cols = slice(c * CHUNK, (c + 1) * CHUNK)
            zh = ps.tile([P, PACK, CHUNK], F32, name="zh%d" % c)
            for t in range(PACK):
                nc.tensor.matmul_mx(out=zh[:, t, :], lhsT=w_codes[:, t, :].bitcast(FP8X4), lhsT_scale=w_scales[:, t, :],
                                    rhs=tab_w[:, cols].bitcast(FP4X4), rhs_scale=tab_s[:, cols], start=True, stop=True)
            nc.scalar.activation(ht[:, c, :, :], zh[:].rearrange("p t n -> p n t"), ACT.Tanh)

        key_s = tile("key_s", [P, I], U8, "tab_scale_pool")
        nc.vector.tensor_copy(key_s[:], key_scale_pool[:].indirect(offsets[:]))
        key_w = tile("key_w", [P, I], U16, "key_scale_pool")
        nc.vector.tensor_copy(key_w[:], key_word_pool[:].indirect(offsets[:]))
        a = ps.tile([P, I], F32, name="a")
        nc.tensor.matmul_mx(out=a[:], lhsT=q_codes[:].bitcast(FP8X4), lhsT_scale=q_scales[:],
                            rhs=key_w[:].bitcast(FP4X4), rhs_scale=key_s[:], start=True, stop=True)

        half_tanh = tile("half_tanh", [P, I], F32)
        abs_tanh = tile("abs_tanh", [P, I], F32)
        relu_x = tile("relu_x", [P, I], F32)
        log_sig = tile("log_sig", [P, I], F32)
        relu_sum = tile("relu_sum", [P, 1], F32)
        log_sum = tile("log_sum", [P, 1], F32)
        nc.scalar.activation(half_tanh[:], a[:], ACT.Tanh, bias=neg_half_th[:], scale=0.5)
        nc.scalar.activation(abs_tanh[:], half_tanh[:], ACT.Abs)
        nc.scalar.activation(log_sig[:], abs_tanh[:], ACT.Ln, bias=0.5, scale=0.5, accum_out=log_sum[:])
        sig512 = tile("sig512", [P, I], F32, "abs_tanh")
        nc.scalar.activation(sig512[:], half_tanh[:], ACT.Identity, bias=256.0, scale=256.0)

        g_bf = tile("g_bf", [P, Q, PACK], BF16)
        nc.gpsimd.tensor_copy(g_bf[:], g_raw[:].rearrange("p j c -> p c j"))
        g_codes = overlaid("g_codes", [P, Q], U32, 0)
        g_scales = tile("g_scales", [P, Q], U8)
        nc.vector.quantize_mx(out=g_codes[:].bitcast(FP8X4), scales=g_scales[:],
                              in_=g_bf[:].rearrange("p c j -> p (c j)"))

        c0 = ps.tile([P, I], F32, name="c0")
        scale_by_place = feature_scale[:].unsqueeze(1).to_broadcast([P, CHUNK, PACK])
        hs = [overlaid("hs%d" % c, [P, CHUNK, PACK], BF16, 4 * Q + 2 * PACK * CHUNK * c)[:] for c in range(CHUNKS)]

        def scale_chunk(c):
            nc.vector.tensor_tensor(hs[c], ht[:, c, :, :], scale_by_place, ALU.mult)

        def multiply_chunk(c):
            h_codes = tile("h_codes%d" % c, [P, CHUNK], U32)
            h_scales = tile("h_scales%d" % c, [P, CHUNK], U8)
            nc.vector.quantize_mx(out=h_codes[:].bitcast(FP8X4), scales=h_scales[:],
                                  in_=hs[c].rearrange("p n t -> p (n t)"))
            nc.tensor.matmul_mx(out=c0[:, c * CHUNK:(c + 1) * CHUNK], lhsT=g_codes[:].bitcast(FP8X4),
                                lhsT_scale=g_scales[:], rhs=h_codes[:].bitcast(FP8X4), rhs_scale=h_scales[:],
                                start=True, stop=True)

        scale_chunk(0)
        for c in range(1, CHUNKS):
            scale_chunk(c)
            multiply_chunk(c - 1)
        multiply_chunk(CHUNKS - 1)

        old_sb = [tile("old_sb%d" % h, [P, T // 2], F32, tag) for h, tag in enumerate(("key_scale_pool", "tab_word_pool"))]
        for h in range(2):
            nc.sync.dma_start(old_sb[h][:], old[:, h * (T // 2):(h + 1) * (T // 2)])

        prod_relu = tile("prod_relu", [P, I], F32)
        prod_log = tile("prod_log", [P, I], F32)
        s_relu = tile("s_relu", [P, 1], F32)
        s_log = tile("s_log", [P, 1], F32)
        z = tile("z", [P, 1], F32)
        rz = tile("rz", [P, 1], F32)
        shift = tile("shift", [P, 1], F32)
        nc.vector.scalar_tensor_tensor(relu_x[:], a[:], th_col[:], zero_col[:].to_broadcast([P, I]), ALU.subtract, ALU.max,
                                       accum_out=relu_sum[:])
        nc.vector.scalar_tensor_tensor(prod_relu[:], c0[:], 1.0, relu_x[:], ALU.mult, ALU.mult, accum_out=s_relu[:])
        nc.vector.tensor_scalar(z[:], relu_sum[:], reserve_col[:], log_sum[:], ALU.add, ALU.subtract)
        nc.vector.scalar_tensor_tensor(prod_log[:], c0[:], 1.0, log_sig[:], ALU.mult, ALU.mult, accum_out=s_log[:])
        nc.vector.reciprocal(rz[:], z[:])
        nc.vector.tensor_scalar(shift[:], s_log[:], s_relu[:], rz[:], ALU.subtract, ALU.mult)
        dp = [tile("dp%d" % h, [P, I // 2], F32) for h in range(2)]
        for h in range(2):
            nc.vector.tensor_scalar(dp[h][:], c0[:, halves[h]], shift[:], rz[:], ALU.add, ALU.mult)
        for h in range(2):
            nc.vector.tensor_tensor(window[:].indirect(list_halves[h]), dp[h][:],
                                    sig512[:, halves[h]], ALU.mult)
        for c, width in enumerate(OUT_COLS):
            cols = slice(sum(OUT_COLS[:c]), sum(OUT_COLS[:c + 1]))
            result = tile("result%d" % c, [P, width], F32)
            nc.vector.tensor_tensor(result[:], window[:, cols], old_sb[cols.start // (T // 2)][:, cols.start % (T // 2):(cols.stop - 1) % (T // 2) + 1], ALU.add)
            nc.sync.dma_start(out[:, cols], result[:])
